import numpy as np
import ml_dtypes


def mxq(x, axis, fmt="e4m3"):
    dtype, down = {"e4m3": (ml_dtypes.float8_e4m3fn, 7), "e5m2": (ml_dtypes.float8_e5m2, 14)}[fmt]
    v = np.moveaxis(np.asarray(x, np.float32).astype(ml_dtypes.bfloat16).astype(np.float64), axis, -1)
    blocks = v.reshape(v.shape[:-1] + (-1, 32))
    amax = np.abs(blocks).max(-1, keepdims=True)
    byte = np.maximum(np.where(amax > 0, np.frexp(amax)[1] - 1 + 127, 0) - down, 1)
    scale = np.exp2(byte - 127.0)
    codes = (blocks / scale).astype(np.float32).astype(dtype).astype(np.float64)
    return np.moveaxis((codes * scale).reshape(v.shape), -1, axis)


WIDE = False


def mx_kscale(k):
    if not WIDE:
        return np.ones(k)
    levels = np.array([10, -10, 5, -5, 0])
    if k % 512:
        return np.exp2(np.random.permutation(np.resize(levels, k // 32))).repeat(32)
    a = np.empty((k // 512, 16))
    for p in range(k // 512):
        a[p, :8] = np.random.permutation(np.resize(levels, 8))
        for g in range(8):
            far = levels[np.abs(levels - a[p, g]) >= 10]
            a[p, g + 8] = far[np.random.randint(len(far))]
    return np.exp2(a.ravel()).repeat(32)


BF16 = ml_dtypes.bfloat16


def bf(x):
    return np.asarray(x, np.float32).astype(BF16)


def f64(x):
    return np.asarray(x).astype(np.float64)


N, R = 2048, 512


def draw0():
    s = mx_kscale(N)
    J = np.random.standard_normal((N, N)) / s
    m = np.tanh(np.random.standard_normal((N, R))) / np.sqrt(N) * s[:, None]
    b = 0.3 * np.random.standard_normal(N)
    c = (1 + 0.1 * np.random.standard_normal(N)) / s
    return {"J": bf(J),
            "m": bf(m),
            "b": bf(b),
            "c": bf(c)}


def core(J, m, b, c):
    mq = mxq(f64(m), 0, "e4m3")
    h = mxq(f64(J), 1, "e4m3") @ mq
    v = np.tanh(h + f64(b)[:, None])
    g = v * f64(c)[:, None]
    q = mxq(g, 0, "e4m3").T @ mq
    return q


def e4m3fn_bytes(y):
    return np.clip(np.asarray(y, np.float64), -448.0, 448.0).astype(np.float32).astype(ml_dtypes.float8_e4m3fn).view(np.uint8)


def e4m3fn_values(b):
    return np.asarray(b, np.uint8).view(ml_dtypes.float8_e4m3fn).astype(np.float64)


def setup_inputs():
    d = draw0()
    x0 = np.asarray(d['J']).astype(np.float64)
    s = (np.max(np.abs(x0), axis=(0,), keepdims=True) / 448.0).astype(np.float32)
    out = {}
    for k, v in d.items():
        if k == 'J':
            out['J_bytes'] = e4m3fn_bytes(x0 / s.astype(np.float64))
            out['J_scale'] = s
        else:
            out[k] = v
    return out


def reference(J_bytes, J_scale, m, b, c):
    return core(e4m3fn_values(J_bytes) * J_scale.astype(np.float64), m, b, c)

@@ -1,0 +1,283 @@
+from contextlib import ExitStack
+
+import concourse.mybir as mybir
+from concourse.masks import make_identity
+
+N, R = 2048, 512
+P = 128
+F32 = mybir.dt.float32
+BF16 = mybir.dt.bfloat16
+U32 = mybir.dt.uint32
+U8 = mybir.dt.uint8
+FP8 = mybir.dt.float8_e4m3fn
+FP8X4 = mybir.dt.float8_e4m3fn_x4
+ACT = mybir.ActivationFunctionType
+MULT = mybir.AluOpType.mult
+
+FLOPS = 2 * N * N * R + 2 * R * R * N
+
+TILES = 16
+PASSES = 4
+
+
+def tile_spin_glass_overlap_s7_kernel(tc, J_bytes, J_scale, m, b, c, out):
+    nc = tc.nc
+    MX_AT = {5: [0], 6: [1, 2], 7: [3, 4], 8: [5, 6]}
+    for n_late in range(7, TILES):
+        MX_AT[n_late + 2] = [n_late]
+    with ExitStack() as ctx:
+        keep = ctx.enter_context(tc.tile_pool(name="keep", bufs=1))
+        bytes_pool = ctx.enter_context(tc.tile_pool(name="bytes", bufs=TILES))
+        scaled_pool = ctx.enter_context(tc.tile_pool(name="scaled", bufs=5))
+        turned_pool = ctx.enter_context(tc.tile_pool(name="turned", bufs=4))
+        m_pool = ctx.enter_context(tc.tile_pool(name="mstage", bufs=4))
+        stage = ctx.enter_context(tc.tile_pool(name="stage", bufs=4))
+        x_psum = ctx.enter_context(tc.psum_pool(name="xpsum", bufs=2))
+        h_psum = ctx.enter_context(tc.psum_pool(name="hpsum", bufs=2))
+        q_psum = ctx.enter_context(tc.psum_pool(name="qpsum", bufs=4))
+
+        J_rows = J_bytes.rearrange("(G m t) j -> G t m j", m=P, t=4)
+        m_rows = m.rearrange("(g p t) a -> g p t a", p=P, t=4)
+        s_row = J_scale.rearrange("o j -> (o j)")
+
+        warm = keep.tile([P, 1], F32, name="warm")
+        ident = keep.tile([P, P], F32, name="ident")
+        jbytes = {}
+        m_raw = {}
+
+        def load_j(n):
+            jb = bytes_pool.tile([P, N], U8, name="jb")
+            nc.sync.dma_start(out=jb[:], in_=J_rows[n // 4, n % 4])
+            jbytes[n] = jb
+
+        def load_m(g):
+            mr = keep.tile([P, 4, R], BF16, name="mr%d" % g, align_bytes=64)
+            nc.sync.dma_start(out=mr[:], in_=m_rows[g])
+            m_raw[g] = mr
+
+        with tc.manual_schedule():
+            nc.gpsimd.memset(warm[:], 0.0)
+            make_identity(nc, ident[:])
+            nc.scalar.activation(warm[:], warm[:], ACT.Tanh)
+            s_all = keep.tile([P, N], F32, name="s_all")
+            b16 = keep.tile([P, 16], BF16, name="b16")
+            c16 = keep.tile([P, 16], BF16, name="c16")
+
+            for what in "J0 s0 s1 s2 s3 J1 m0 m1 J2 m2 m3 bc".split(" "):
+                if what == "bc":
+                    nc.sync.dma_start(out=b16[:].rearrange("p (G t) -> p G t", t=4), in_=b.rearrange("(G p t) -> p G t", p=P, t=4))
+                    nc.sync.dma_start(out=c16[:].rearrange("p (G t) -> p G t", t=4), in_=c.rearrange("(G p t) -> p G t", p=P, t=4))
+                elif what.startswith("J"):
+                    load_j(int(what.replace("J", "")))
+                elif what.startswith("m"):
+                    load_m(int(what.replace("m", "")))
+                else:
+                    k = int(what.replace("s", ""))
+                    nc.sync.dma_start(out=s_all[:, 512 * k : 512 * (k + 1)], in_=s_row[512 * k : 512 * (k + 1)].partition_broadcast(P))
+            for n in range(TILES):
+                if n not in jbytes:
+                    load_j(n)
+            b32 = keep.tile([P, 16], F32, name="b32")
+            c32 = keep.tile([P, 16], F32, name="c32")
+            nc.gpsimd.tensor_copy(out=b32[:], in_=b16[:])
+            nc.gpsimd.tensor_copy(out=c32[:], in_=c16[:])
+
+            scaled = {}
+            turned = {}
+            jq = {}
+            jqs = {}
+            mi = {}
+            mq = {}
+            mqs = {}
+            planes = {}
+            gi = {}
+            gq = {}
+            gqs = {}
+            vs = {}
+            hs = {}
+            qacc = [q_psum.tile([P, R], F32, name="qacc") for qi in range(4)]
+
+            def copy(which, o, i):
+                if which == "v":
+                    nc.vector.tensor_copy(out=o, in_=i)
+                else:
+                    nc.scalar.copy(o, i)
+
+            def mult(n):
+                js = scaled_pool.tile([P, N], BF16, name="js")
+                scaled[n] = js
+                width = 512 if n == 0 else N
+                for c0 in range(0, N, width):
+                    nc.vector.tensor_tensor(
+                        js[:, c0 : c0 + width], jbytes[n][:, c0 : c0 + width].bitcast(FP8), s_all[:, c0 : c0 + width], op=MULT
+                    )
+
+            def turn(n, h, which="s"):
+                words = scaled[n][:].bitcast(F32)
+                if h == 0:
+                    jt = turned_pool.tile([P, N], BF16, name="jt", align_bytes=64)
+                    turned[n] = jt
+                jt_words = turned[n][:].bitcast(F32)
+                xt = x_psum.tile([P, 4, P], F32, name="xt")
+                for gg in range(2):
+                    for u in range(2):
+                        w0 = 256 * (2 * h + gg)
+                        nc.tensor.transpose(xt[:, 2 * gg + u, :], words[:, w0 + u : w0 + 256 : 2], ident[:])
+                copy(
+                    which,
+                    jt_words[:, 512 * h : 512 * (h + 1)].rearrange("p (g r u) -> p g r u", r=P, u=2),
+                    xt[:].rearrange("p (g u) r -> p g r u", u=2),
+                )
+
+            def quant_j(n, halves=1):
+                if n not in jq:
+                    codes = keep.tile([P, 512], U32, name="jq%d" % n, align_bytes=64)
+                    scl = keep.tile([P, 512], U8, name="jqs%d" % n, align_bytes=64)
+                    jq[n] = codes
+                    jqs[n] = scl
+                w = N // halves
+                for k in range(halves):
+                    nc.vector.quantize_mx(
+                        out=jq[n][:, k * w // 4 : (k + 1) * w // 4].bitcast(FP8X4),
+                        scales=jqs[n][:, k * w // 4 : (k + 1) * w // 4],
+                        in_=turned[n][:, k * w : (k + 1) * w],
+                    )
+
+            def inter_m(g, which):
+                t_mi = m_pool.tile([P, N], BF16, name="t_mi", align_bytes=64)
+                copy(which, t_mi[:].rearrange("p (a t) -> p a t", t=4), m_raw[g][:].rearrange("p t a -> p a t"))
+                mi[g] = t_mi
+
+            def quant_m(g):
+                codes = keep.tile([P, R], U32, name="mq%d" % g, align_bytes=64)
+                scl = keep.tile([P, R], U8, name="mqs%d" % g, align_bytes=64)
+                nc.vector.quantize_mx(out=codes[:].bitcast(FP8X4), scales=scl[:], in_=mi[g][:])
+                mq[g] = codes
+                mqs[g] = scl
+
+            def field(n):
+                h = h_psum.tile([P, R], F32, name="h")
+                hs[n] = h
+                for g in range(PASSES):
+                    cols = slice(P * g, P * (g + 1))
+                    nc.tensor.matmul_mx(
+                        out=h[:],
+                        lhsT=jq[n][:, cols].bitcast(FP8X4),
+                        lhsT_scale=jqs[n][:, cols],
+                        rhs=mq[g][:].bitcast(FP8X4),
+                        rhs_scale=mqs[g][:],
+                        start=(g == 0),
+                        stop=(g == PASSES - 1),
+                    )
+
+            def tanh(n, parts=1):
+                v = stage.tile([P, R], F32, name="v")
+                vs[n] = v
+                w = R // parts
+                for k in range(parts):
+                    nc.scalar.activation(v[:, k * w : (k + 1) * w], hs[n][:, k * w : (k + 1) * w], ACT.Tanh, bias=b32[:, n : n + 1])
+
+            def weigh(n, which="s", parts=1):
+                v = vs[n]
+                if n // 4 not in planes:
+                    planes[n // 4] = stage.tile([P, 4, R], BF16, name="pl", align_bytes=64)
+                w = R // parts
+                for k in range(parts):
+                    o = planes[n // 4][:, n % 4, k * w : (k + 1) * w]
+                    i = v[:, k * w : (k + 1) * w]
+                    if which == "s":
+                        nc.scalar.activation(o, i, ACT.Copy, scale=c32[:, n : n + 1])
+                    else:
+                        nc.vector.tensor_scalar(o, i, c32[:, n : n + 1], None, op0=MULT)
+
+            def inter_g(G, q, which):
+                t_gi = stage.tile([P, 512], BF16, name="t_gi", align_bytes=64)
+                copy(
+                    which,
+                    t_gi[:].rearrange("p (a t) -> p a t", t=4),
+                    planes[G][:, :, P * q : P * (q + 1)].rearrange("p t a -> p a t"),
+                )
+                gi[G, q] = t_gi
+
+            def quant_g(G, q):
+                codes = stage.tile([P, P], U32, name="gcodes", align_bytes=64)
+                scl = stage.tile([P, P], U8, name="gscl", align_bytes=64)
+                nc.vector.quantize_mx(out=codes[:].bitcast(FP8X4), scales=scl[:], in_=gi[G, q][:])
+                gq[G, q] = codes
+                gqs[G, q] = scl
+
+            def overlap(G, q):
+                nc.tensor.matmul_mx(
+                    out=qacc[q][:],
+                    lhsT=gq[G, q][:].bitcast(FP8X4),
+                    lhsT_scale=gqs[G, q][:],
+                    rhs=mq[G][:].bitcast(FP8X4),
+                    rhs_scale=mqs[G][:],
+                    start=(G == 0),
+                    stop=(G == 3),
+                )
+
+            MI_AT = {0:0,1:1,2:2,3:3}
+            GI_V = [1,3]
+            mult(0)
+            mult(1)
+            g_start = {}
+            for s in range(0, 15):
+                if s == 14:
+                    quant_j(s - 1)
+                if s + 2 < TILES:
+                    mult(s + 2)
+                turn(s, 0)
+                turn(s, 1)
+                if 0 <= s - 1 and s != 14:
+                    quant_j(s - 1)
+                for g in range(PASSES):
+                    if MI_AT[g] == s:
+                        inter_m(g, "s")
+                    if MI_AT[g] + 1 == s:
+                        quant_m(g)
+                for n in MX_AT.get(s, []):
+                    field(n)
+                    tanh(n)
+                    weigh(n)
+                for G in range(3):
+                    if G in g_start:
+                        k = s - g_start[G]
+                        if 1 <= k <= 4:
+                            inter_g(G, k - 1, "v" if (k - 1) in GI_V else "s")
+                        if 2 <= k <= 5:
+                            quant_g(G, k - 2)
+                            overlap(G, k - 2)
+                for n in MX_AT.get(s, []):
+                    if n % 4 == 3:
+                        g_start[n // 4] = s
+            field(13)
+            quant_j(14)
+            turn(15, 0)
+            tanh(13)
+            turn(15, 1, "v")
+            weigh(13, "v")
+            field(14)
+            quant_j(15)
+            tanh(14)
+            field(15)
+            for q in range(4):
+                if (2, q) not in gi:
+                    inter_g(2, q, "v")
+            weigh(14, "v")
+            tanh(15, 2)
+            for q in range(4):
+                if (2, q) not in gq:
+                    quant_g(2, q)
+                    overlap(2, q)
+            weigh(15, "v", 2)
+            for q in range(5):
+                if q < 4:
+                    inter_g(3, q, "vs"[q % 2])
+                if q > 0:
+                    quant_g(3, q - 1)
+                    overlap(3, q - 1)
+            for q in range(4):
+                res = stage.tile([P, R], F32, name="res")
+                copy("sv"[q % 2], res[:], qacc[q][:])
+                nc.sync.dma_start(out=out[P * q : P * (q + 1), :], in_=res[:])

@@ -3,281 +3,295 @@ from contextlib import ExitStack
 import concourse.mybir as mybir
 from concourse.masks import make_identity
 
-N, R = 2048, 512
+SITES, REPLICAS = 2048, 512
+FLOPS = 2 * SITES * SITES * REPLICAS + 2 * REPLICAS * REPLICAS * SITES
+
 P = 128
+PACK = 4
+PASSES = SITES // (P * PACK)
+TILES = SITES // P
+GROUPS = TILES // PACK
+CHUNKS = REPLICAS // P
+PASS_COLS = PACK * P
+WORDS = PASS_COLS // 2
+NEAR = 4
+
 F32 = mybir.dt.float32
 BF16 = mybir.dt.bfloat16
 U32 = mybir.dt.uint32
 U8 = mybir.dt.uint8
 FP8 = mybir.dt.float8_e4m3fn
 FP8X4 = mybir.dt.float8_e4m3fn_x4
-ACT = mybir.ActivationFunctionType
 MULT = mybir.AluOpType.mult
+COPY = mybir.ActivationFunctionType.Copy
+TANH = mybir.ActivationFunctionType.Tanh
 
-FLOPS = 2 * N * N * R + 2 * R * R * N
+LAG_MULTIPLY = -3.05
+LAG_TURN = 0.0
+LAG_SECOND_HALF = 0.35
+LAG_QUANTISE = 1.3
+LAG_FIELD = 4.75
+LAG_TANH = 4.95
+LAG_WEIGH = 6.9
+LAG_INTERLEAVE = 8.4
+LAG_QUANTISE_G = 10.4
+LAG_OVERLAP = 15.8
+CHUNK_STEP = 1.15
+SLOT_INTERLEAVE_M = (-1.75, 1.8, 0.75, 1.65)
+LAG_QUANTISE_M = 0.75
+SLOT_END = 1000.0
 
-TILES = 16
-PASSES = 4
+FIRST_TILE_WEIGHED_ON_VECTOR = 8
+CHUNKS_INTERLEAVED_ON_VECTOR = (1, 2)
+LAST_CHUNKS_INTERLEAVED_ON_VECTOR = (0, 3)
 
 
 def tile_spin_glass_overlap_s7_kernel(tc, J_bytes, J_scale, m, b, c, out):
     nc = tc.nc
-    MX_AT = {5: [0], 6: [1, 2], 7: [3, 4], 8: [5, 6]}
-    for n_late in range(7, TILES):
-        MX_AT[n_late + 2] = [n_late]
     with ExitStack() as ctx:
         keep = ctx.enter_context(tc.tile_pool(name="keep", bufs=1))
-        bytes_pool = ctx.enter_context(tc.tile_pool(name="bytes", bufs=TILES))
+        code_pool = ctx.enter_context(tc.tile_pool(name="codes", bufs=TILES))
         scaled_pool = ctx.enter_context(tc.tile_pool(name="scaled", bufs=5))
-        turned_pool = ctx.enter_context(tc.tile_pool(name="turned", bufs=4))
-        m_pool = ctx.enter_context(tc.tile_pool(name="mstage", bufs=4))
-        stage = ctx.enter_context(tc.tile_pool(name="stage", bufs=4))
-        x_psum = ctx.enter_context(tc.psum_pool(name="xpsum", bufs=2))
-        h_psum = ctx.enter_context(tc.psum_pool(name="hpsum", bufs=2))
-        q_psum = ctx.enter_context(tc.psum_pool(name="qpsum", bufs=4))
+        turned_pool = ctx.enter_context(tc.tile_pool(name="turned", bufs=5))
+        m_pool = ctx.enter_context(tc.tile_pool(name="m", bufs=PASSES))
+        group_pool = ctx.enter_context(tc.tile_pool(name="group", bufs=GROUPS))
+        chunk_pool = ctx.enter_context(tc.tile_pool(name="chunk", bufs=GROUPS * CHUNKS))
+        stage = ctx.enter_context(tc.tile_pool(name="stage", bufs=5))
+        turn_psum = ctx.enter_context(tc.psum_pool(name="turn_psum", bufs=2))
+        field_psum = ctx.enter_context(tc.psum_pool(name="field_psum", bufs=2))
+        overlap_psum = ctx.enter_context(tc.psum_pool(name="overlap_psum", bufs=CHUNKS))
 
-        J_rows = J_bytes.rearrange("(G m t) j -> G t m j", m=P, t=4)
-        m_rows = m.rearrange("(g p t) a -> g p t a", p=P, t=4)
-        s_row = J_scale.rearrange("o j -> (o j)")
+        ctx.enter_context(tc.manual_schedule())
 
         warm = keep.tile([P, 1], F32, name="warm")
+        nc.gpsimd.memset(warm[:], 0.0)
+        nc.scalar.activation(warm[:], warm[:], TANH)
         ident = keep.tile([P, P], F32, name="ident")
-        jbytes = {}
+        make_identity(nc, ident[:])
+
+        scales = keep.tile([P, SITES], F32, name="scales")
+        b16 = keep.tile([P, TILES], BF16, name="b16")
+        c16 = keep.tile([P, TILES], BF16, name="c16")
+        b32 = keep.tile([P, TILES], F32, name="b32")
+        c32 = keep.tile([P, TILES], F32, name="c32")
+
+        j_codes = {}
         m_raw = {}
+        m_mixed = {}
+        m_mx, m_mx_scale = {}, {}
+        j_scaled = {}
+        words_psum = {}
+        j_turned = {}
+        j_mx, j_mx_scale = {}, {}
+        h_psum = {}
+        v = {}
+        g = {}
+        g_mixed = {}
+        g_mx, g_mx_scale = {}, {}
 
         def load_j(n):
-            jb = bytes_pool.tile([P, N], U8, name="jb")
-            nc.sync.dma_start(out=jb[:], in_=J_rows[n // 4, n % 4])
-            jbytes[n] = jb
+            tile = code_pool.tile([P, SITES], U8, name="j_bytes")
+            rows = J_bytes.rearrange("(G p t) j -> G t p j", p=P, t=PACK)
+            nc.sync.dma_start(out=tile[:], in_=rows[n // PACK, n % PACK])
+            j_codes[n] = tile
 
-        def load_m(g):
-            mr = keep.tile([P, 4, R], BF16, name="mr%d" % g, align_bytes=64)
-            nc.sync.dma_start(out=mr[:], in_=m_rows[g])
-            m_raw[g] = mr
+        def load_scales(part):
+            cols = slice(part * SITES // 4, (part + 1) * SITES // 4)
+            row = J_scale.rearrange("o j -> (o j)")
+            nc.sync.dma_start(out=scales[:, cols], in_=row[cols].partition_broadcast(P))
 
-        with tc.manual_schedule():
-            nc.gpsimd.memset(warm[:], 0.0)
-            make_identity(nc, ident[:])
-            nc.scalar.activation(warm[:], warm[:], ACT.Tanh)
-            s_all = keep.tile([P, N], F32, name="s_all")
-            b16 = keep.tile([P, 16], BF16, name="b16")
-            c16 = keep.tile([P, 16], BF16, name="c16")
+        def load_m(k):
+            tile = m_pool.tile([P, PACK, REPLICAS], BF16, name="m_rows", align_bytes=64)
+            nc.sync.dma_start(out=tile[:], in_=m.rearrange("(k p t) a -> k p t a", p=P, t=PACK)[k])
+            m_raw[k] = tile
 
-            for what in "J0 s0 s1 s2 s3 J1 m0 m1 J2 m2 m3 bc".split(" "):
-                if what == "bc":
-                    nc.sync.dma_start(out=b16[:].rearrange("p (G t) -> p G t", t=4), in_=b.rearrange("(G p t) -> p G t", p=P, t=4))
-                    nc.sync.dma_start(out=c16[:].rearrange("p (G t) -> p G t", t=4), in_=c.rearrange("(G p t) -> p G t", p=P, t=4))
-                elif what.startswith("J"):
-                    load_j(int(what.replace("J", "")))
-                elif what.startswith("m"):
-                    load_m(int(what.replace("m", "")))
-                else:
-                    k = int(what.replace("s", ""))
-                    nc.sync.dma_start(out=s_all[:, 512 * k : 512 * (k + 1)], in_=s_row[512 * k : 512 * (k + 1)].partition_broadcast(P))
-            for n in range(TILES):
-                if n not in jbytes:
-                    load_j(n)
-            b32 = keep.tile([P, 16], F32, name="b32")
-            c32 = keep.tile([P, 16], F32, name="c32")
-            nc.gpsimd.tensor_copy(out=b32[:], in_=b16[:])
-            nc.gpsimd.tensor_copy(out=c32[:], in_=c16[:])
+        def load_sites(tile16, vector):
+            nc.sync.dma_start(
+                out=tile16[:].rearrange("p (G t) -> p G t", t=PACK),
+                in_=vector.rearrange("(G p t) -> p G t", p=P, t=PACK),
+            )
 
-            scaled = {}
-            turned = {}
-            jq = {}
-            jqs = {}
-            mi = {}
-            mq = {}
-            mqs = {}
-            planes = {}
-            gi = {}
-            gq = {}
-            gqs = {}
-            vs = {}
-            hs = {}
-            qacc = [q_psum.tile([P, R], F32, name="qacc") for qi in range(4)]
+        load_j(0)
+        for part in range(4):
+            load_scales(part)
+        load_j(1)
+        load_m(0)
+        load_m(1)
+        load_j(2)
+        load_m(2)
+        load_m(3)
+        load_sites(b16, b)
+        load_sites(c16, c)
+        for n in range(3, TILES):
+            load_j(n)
+        nc.gpsimd.tensor_copy(out=b32[:], in_=b16[:])
+        nc.gpsimd.tensor_copy(out=c32[:], in_=c16[:])
 
-            def copy(which, o, i):
-                if which == "v":
-                    nc.vector.tensor_copy(out=o, in_=i)
-                else:
-                    nc.scalar.copy(o, i)
+        def copy(out_ap, in_ap, on_vector):
+            if on_vector:
+                nc.vector.tensor_copy(out=out_ap, in_=in_ap)
+            else:
+                nc.scalar.copy(out_ap, in_ap)
 
-            def mult(n):
-                js = scaled_pool.tile([P, N], BF16, name="js")
-                scaled[n] = js
-                width = 512 if n == 0 else N
-                for c0 in range(0, N, width):
-                    nc.vector.tensor_tensor(
-                        js[:, c0 : c0 + width], jbytes[n][:, c0 : c0 + width].bitcast(FP8), s_all[:, c0 : c0 + width], op=MULT
-                    )
+        def interleave(mixed, rows, on_vector):
+            copy(
+                mixed.rearrange("p (w i t) -> p w t i", i=NEAR, t=PACK),
+                rows.rearrange("p t (w i) -> p w t i", i=NEAR),
+                on_vector,
+            )
 
-            def turn(n, h, which="s"):
-                words = scaled[n][:].bitcast(F32)
-                if h == 0:
-                    jt = turned_pool.tile([P, N], BF16, name="jt", align_bytes=64)
-                    turned[n] = jt
-                jt_words = turned[n][:].bitcast(F32)
-                xt = x_psum.tile([P, 4, P], F32, name="xt")
-                for gg in range(2):
-                    for u in range(2):
-                        w0 = 256 * (2 * h + gg)
-                        nc.tensor.transpose(xt[:, 2 * gg + u, :], words[:, w0 + u : w0 + 256 : 2], ident[:])
-                copy(
-                    which,
-                    jt_words[:, 512 * h : 512 * (h + 1)].rearrange("p (g r u) -> p g r u", r=P, u=2),
-                    xt[:].rearrange("p (g u) r -> p g r u", u=2),
+        def quantise(codes, code_scales, mixed):
+            nc.vector.quantize_mx(out=codes.bitcast(FP8X4), scales=code_scales, in_=mixed)
+
+        def matmul_mx(acc, lhsT, lhsT_scale, rhs, rhs_scale, start, stop):
+            nc.tensor.matmul_mx(
+                out=acc,
+                lhsT=lhsT.bitcast(FP8X4),
+                lhsT_scale=lhsT_scale,
+                rhs=rhs.bitcast(FP8X4),
+                rhs_scale=rhs_scale,
+                start=start,
+                stop=stop,
+            )
+
+        def interleave_m(k):
+            tile = m_pool.tile([P, PACK * REPLICAS], BF16, name="m_mixed", align_bytes=64)
+            interleave(tile[:], m_raw[k][:], on_vector=False)
+            m_mixed[k] = tile
+
+        def quantise_m(k):
+            codes = m_pool.tile([P, REPLICAS], U32, name="m_codes", align_bytes=64)
+            code_scales = m_pool.tile([P, REPLICAS], U8, name="m_scales", align_bytes=64)
+            quantise(codes[:], code_scales[:], m_mixed[k][:])
+            m_mx[k], m_mx_scale[k] = codes, code_scales
+
+        def multiply(n):
+            tile = scaled_pool.tile([P, SITES], BF16, name="j_scaled")
+            parts = 4 if n == 0 else 1
+            for part in range(parts):
+                cols = slice(part * SITES // parts, (part + 1) * SITES // parts)
+                nc.vector.tensor_tensor(tile[:, cols], j_codes[n][:, cols].bitcast(FP8), scales[:, cols], op=MULT)
+            j_scaled[n] = tile
+
+        def turn(n, half):
+            words = j_scaled[n][:].bitcast(F32)
+            bank = turn_psum.tile([P, 4, P], F32, name="turn_bank")
+            for k in range(2):
+                first = (2 * half + k) * WORDS
+                for u in range(2):
+                    nc.tensor.transpose(bank[:, 2 * k + u, :], words[:, first + u : first + WORDS : 2], ident[:])
+            words_psum[n, half] = bank
+
+        def empty(n, half):
+            if half == 0:
+                tile = turned_pool.tile([P, PASSES * PASS_COLS], BF16, name="j_turned", align_bytes=64)
+                j_turned[n] = tile
+            words = j_turned[n][:].bitcast(F32)[:, half * 2 * WORDS : (half + 1) * 2 * WORDS]
+            nc.scalar.copy(
+                words.rearrange("p (k r u) -> p k r u", r=P, u=2),
+                words_psum[n, half][:].rearrange("p (k u) r -> p k r u", u=2),
+            )
+
+        def quantise_j(n):
+            codes = code_pool.tile([P, PASSES * P], U32, name="j_codes", align_bytes=64)
+            code_scales = code_pool.tile([P, PASSES * P], U8, name="j_scales", align_bytes=64)
+            quantise(codes[:], code_scales[:], j_turned[n][:])
+            j_mx[n], j_mx_scale[n] = codes, code_scales
+
+        def field(n):
+            bank = field_psum.tile([P, REPLICAS], F32, name="field_bank")
+            for k in range(PASSES):
+                rows = slice(k * P, (k + 1) * P)
+                matmul_mx(
+                    bank[:],
+                    j_mx[n][:, rows],
+                    j_mx_scale[n][:, rows],
+                    m_mx[k][:],
+                    m_mx_scale[k][:],
+                    start=(k == 0),
+                    stop=(k == PASSES - 1),
                 )
+            h_psum[n] = bank
 
-            def quant_j(n, halves=1):
-                if n not in jq:
-                    codes = keep.tile([P, 512], U32, name="jq%d" % n, align_bytes=64)
-                    scl = keep.tile([P, 512], U8, name="jqs%d" % n, align_bytes=64)
-                    jq[n] = codes
-                    jqs[n] = scl
-                w = N // halves
-                for k in range(halves):
-                    nc.vector.quantize_mx(
-                        out=jq[n][:, k * w // 4 : (k + 1) * w // 4].bitcast(FP8X4),
-                        scales=jqs[n][:, k * w // 4 : (k + 1) * w // 4],
-                        in_=turned[n][:, k * w : (k + 1) * w],
-                    )
+        def replicas(part, parts):
+            return slice(part * REPLICAS // parts, (part + 1) * REPLICAS // parts)
 
-            def inter_m(g, which):
-                t_mi = m_pool.tile([P, N], BF16, name="t_mi", align_bytes=64)
-                copy(which, t_mi[:].rearrange("p (a t) -> p a t", t=4), m_raw[g][:].rearrange("p t a -> p a t"))
-                mi[g] = t_mi
+        def apply_tanh(n, part, parts):
+            if part == 0:
+                tile = stage.tile([P, REPLICAS], F32, name="v")
+                v[n] = tile
+            cols = replicas(part, parts)
+            nc.scalar.activation(v[n][:, cols], h_psum[n][:, cols], TANH, bias=b32[:, n : n + 1])
 
-            def quant_m(g):
-                codes = keep.tile([P, R], U32, name="mq%d" % g, align_bytes=64)
-                scl = keep.tile([P, R], U8, name="mqs%d" % g, align_bytes=64)
-                nc.vector.quantize_mx(out=codes[:].bitcast(FP8X4), scales=scl[:], in_=mi[g][:])
-                mq[g] = codes
-                mqs[g] = scl
+        def weigh(n, part, parts):
+            group, t = n // PACK, n % PACK
+            if group not in g:
+                tile = group_pool.tile([P, PACK, REPLICAS], BF16, name="g", align_bytes=64)
+                g[group] = tile
+            cols = replicas(part, parts)
+            if n >= FIRST_TILE_WEIGHED_ON_VECTOR:
+                nc.vector.tensor_scalar(g[group][:, t, cols], v[n][:, cols], c32[:, n : n + 1], None, op0=MULT)
+            else:
+                nc.scalar.activation(g[group][:, t, cols], v[n][:, cols], COPY, scale=c32[:, n : n + 1])
 
-            def field(n):
-                h = h_psum.tile([P, R], F32, name="h")
-                hs[n] = h
-                for g in range(PASSES):
-                    cols = slice(P * g, P * (g + 1))
-                    nc.tensor.matmul_mx(
-                        out=h[:],
-                        lhsT=jq[n][:, cols].bitcast(FP8X4),
-                        lhsT_scale=jqs[n][:, cols],
-                        rhs=mq[g][:].bitcast(FP8X4),
-                        rhs_scale=mqs[g][:],
-                        start=(g == 0),
-                        stop=(g == PASSES - 1),
-                    )
+        def interleave_g(group, chunk, on_vector):
+            tile = chunk_pool.tile([P, PACK * P], BF16, name="g_mixed", align_bytes=64)
+            interleave(tile[:], g[group][:, :, chunk * P : (chunk + 1) * P], on_vector)
+            g_mixed[group, chunk] = tile
 
-            def tanh(n, parts=1):
-                v = stage.tile([P, R], F32, name="v")
-                vs[n] = v
-                w = R // parts
-                for k in range(parts):
-                    nc.scalar.activation(v[:, k * w : (k + 1) * w], hs[n][:, k * w : (k + 1) * w], ACT.Tanh, bias=b32[:, n : n + 1])
+        def quantise_g(group, chunk):
+            codes = chunk_pool.tile([P, P], U32, name="g_codes", align_bytes=64)
+            code_scales = chunk_pool.tile([P, P], U8, name="g_scales", align_bytes=64)
+            quantise(codes[:], code_scales[:], g_mixed[group, chunk][:])
+            g_mx[group, chunk], g_mx_scale[group, chunk] = codes, code_scales
 
-            def weigh(n, which="s", parts=1):
-                v = vs[n]
-                if n // 4 not in planes:
-                    planes[n // 4] = stage.tile([P, 4, R], BF16, name="pl", align_bytes=64)
-                w = R // parts
-                for k in range(parts):
-                    o = planes[n // 4][:, n % 4, k * w : (k + 1) * w]
-                    i = v[:, k * w : (k + 1) * w]
-                    if which == "s":
-                        nc.scalar.activation(o, i, ACT.Copy, scale=c32[:, n : n + 1])
-                    else:
-                        nc.vector.tensor_scalar(o, i, c32[:, n : n + 1], None, op0=MULT)
+        overlap_banks = [overlap_psum.tile([P, REPLICAS], F32, name="overlap_bank") for chunk in range(CHUNKS)]
 
-            def inter_g(G, q, which):
-                t_gi = stage.tile([P, 512], BF16, name="t_gi", align_bytes=64)
-                copy(
-                    which,
-                    t_gi[:].rearrange("p (a t) -> p a t", t=4),
-                    planes[G][:, :, P * q : P * (q + 1)].rearrange("p t a -> p a t"),
-                )
-                gi[G, q] = t_gi
+        def overlap(group, chunk):
+            matmul_mx(
+                overlap_banks[chunk][:],
+                g_mx[group, chunk][:],
+                g_mx_scale[group, chunk][:],
+                m_mx[group][:],
+                m_mx_scale[group][:],
+                start=(group == 0),
+                stop=(group == GROUPS - 1),
+            )
 
-            def quant_g(G, q):
-                codes = stage.tile([P, P], U32, name="gcodes", align_bytes=64)
-                scl = stage.tile([P, P], U8, name="gscl", align_bytes=64)
-                nc.vector.quantize_mx(out=codes[:].bitcast(FP8X4), scales=scl[:], in_=gi[G, q][:])
-                gq[G, q] = codes
-                gqs[G, q] = scl
+        def finish(chunk):
+            result = stage.tile([P, REPLICAS], F32, name="result")
+            copy(result[:], overlap_banks[chunk][:], on_vector=(chunk % 2 == 1))
+            nc.sync.dma_start(out=out[chunk * P : (chunk + 1) * P, :], in_=result[:])
 
-            def overlap(G, q):
-                nc.tensor.matmul_mx(
-                    out=qacc[q][:],
-                    lhsT=gq[G, q][:].bitcast(FP8X4),
-                    lhsT_scale=gqs[G, q][:],
-                    rhs=mq[G][:].bitcast(FP8X4),
-                    rhs_scale=mqs[G][:],
-                    start=(G == 0),
-                    stop=(G == 3),
-                )
+        tasks = []
 
-            MI_AT = {0:0,1:1,2:2,3:3}
-            GI_V = [1,3]
-            mult(0)
-            mult(1)
-            g_start = {}
-            for s in range(0, 15):
-                if s == 14:
-                    quant_j(s - 1)
-                if s + 2 < TILES:
-                    mult(s + 2)
-                turn(s, 0)
-                turn(s, 1)
-                if 0 <= s - 1 and s != 14:
-                    quant_j(s - 1)
-                for g in range(PASSES):
-                    if MI_AT[g] == s:
-                        inter_m(g, "s")
-                    if MI_AT[g] + 1 == s:
-                        quant_m(g)
-                for n in MX_AT.get(s, []):
-                    field(n)
-                    tanh(n)
-                    weigh(n)
-                for G in range(3):
-                    if G in g_start:
-                        k = s - g_start[G]
-                        if 1 <= k <= 4:
-                            inter_g(G, k - 1, "v" if (k - 1) in GI_V else "s")
-                        if 2 <= k <= 5:
-                            quant_g(G, k - 2)
-                            overlap(G, k - 2)
-                for n in MX_AT.get(s, []):
-                    if n % 4 == 3:
-                        g_start[n // 4] = s
-            field(13)
-            quant_j(14)
-            turn(15, 0)
-            tanh(13)
-            turn(15, 1, "v")
-            weigh(13, "v")
-            field(14)
-            quant_j(15)
-            tanh(14)
-            field(15)
-            for q in range(4):
-                if (2, q) not in gi:
-                    inter_g(2, q, "v")
-            weigh(14, "v")
-            tanh(15, 2)
-            for q in range(4):
-                if (2, q) not in gq:
-                    quant_g(2, q)
-                    overlap(2, q)
-            weigh(15, "v", 2)
-            for q in range(5):
-                if q < 4:
-                    inter_g(3, q, "vs"[q % 2])
-                if q > 0:
-                    quant_g(3, q - 1)
-                    overlap(3, q - 1)
-            for q in range(4):
-                res = stage.tile([P, R], F32, name="res")
-                copy("sv"[q % 2], res[:], qacc[q][:])
-                nc.sync.dma_start(out=out[P * q : P * (q + 1), :], in_=res[:])
+        def at(slot, task, *args):
+            tasks.append((slot, len(tasks), task, args))
+
+        for k in range(PASSES):
+            at(SLOT_INTERLEAVE_M[k], interleave_m, k)
+            at(SLOT_INTERLEAVE_M[k] + LAG_QUANTISE_M, quantise_m, k)
+        for n in range(TILES):
+            at(n + LAG_MULTIPLY, multiply, n)
+            for half in range(2):
+                at(n + LAG_TURN + half * LAG_SECOND_HALF, turn, n, half)
+                at(n + LAG_TURN + half * LAG_SECOND_HALF, empty, n, half)
+            at(n + LAG_QUANTISE, quantise_j, n)
+            at(n + LAG_FIELD, field, n)
+            parts = 2 if n == TILES - 1 else 1
+            for part in range(parts):
+                at(n + LAG_TANH, apply_tanh, n, part, parts)
+                at(n + LAG_WEIGH, weigh, n, part, parts)
+        for chunk in range(CHUNKS):
+            for group in range(GROUPS - 1):
+                slot = group * PACK + PACK - 1 + chunk * CHUNK_STEP
+                at(slot + LAG_INTERLEAVE, interleave_g, group, chunk, chunk in CHUNKS_INTERLEAVED_ON_VECTOR)
+                at(slot + LAG_QUANTISE_G, quantise_g, group, chunk)
+                at(slot + LAG_OVERLAP, overlap, group, chunk)
+            at(SLOT_END, interleave_g, GROUPS - 1, chunk, chunk in LAST_CHUNKS_INTERLEAVED_ON_VECTOR)
+            at(SLOT_END + 1, quantise_g, GROUPS - 1, chunk)
+            at(SLOT_END + 1, overlap, GROUPS - 1, chunk)
+        for chunk in range(CHUNKS):
+            at(SLOT_END + 2, finish, chunk)
+        for slot, order, task, args in sorted(tasks, key=lambda entry: entry[:2]):
+            task(*args)

from contextlib import ExitStack

import concourse.mybir as mybir
from concourse.masks import make_identity

SITES, REPLICAS = 2048, 512
FLOPS = 2 * SITES * SITES * REPLICAS + 2 * REPLICAS * REPLICAS * SITES

P = 128
PACK = 4
PASSES = SITES // (P * PACK)
TILES = SITES // P
GROUPS = TILES // PACK
CHUNKS = REPLICAS // P
PASS_COLS = PACK * P
WORDS = PASS_COLS // 2
NEAR = 4

F32 = mybir.dt.float32
BF16 = mybir.dt.bfloat16
U32 = mybir.dt.uint32
U8 = mybir.dt.uint8
FP8 = mybir.dt.float8_e4m3fn
FP8X4 = mybir.dt.float8_e4m3fn_x4
MULT = mybir.AluOpType.mult
COPY = mybir.ActivationFunctionType.Copy
TANH = mybir.ActivationFunctionType.Tanh

LAG_MULTIPLY = -3.05
LAG_TURN = 0.0
LAG_SECOND_HALF = 0.35
LAG_QUANTISE = 1.3
LAG_FIELD = 4.75
LAG_TANH = 4.95
LAG_WEIGH = 6.9
LAG_INTERLEAVE = 8.4
LAG_QUANTISE_G = 10.4
LAG_OVERLAP = 15.8
CHUNK_STEP = 1.15
SLOT_INTERLEAVE_M = (-1.75, 1.8, 0.75, 1.65)
LAG_QUANTISE_M = 0.75
SLOT_END = 1000.0

FIRST_TILE_WEIGHED_ON_VECTOR = 8
CHUNKS_INTERLEAVED_ON_VECTOR = (1, 2)
LAST_CHUNKS_INTERLEAVED_ON_VECTOR = (0, 3)


def tile_spin_glass_overlap_s7_kernel(tc, J_bytes, J_scale, m, b, c, out):
    nc = tc.nc
    with ExitStack() as ctx:
        keep = ctx.enter_context(tc.tile_pool(name="keep", bufs=1))
        code_pool = ctx.enter_context(tc.tile_pool(name="codes", bufs=TILES))
        scaled_pool = ctx.enter_context(tc.tile_pool(name="scaled", bufs=5))
        turned_pool = ctx.enter_context(tc.tile_pool(name="turned", bufs=5))
        m_pool = ctx.enter_context(tc.tile_pool(name="m", bufs=PASSES))
        group_pool = ctx.enter_context(tc.tile_pool(name="group", bufs=GROUPS))
        chunk_pool = ctx.enter_context(tc.tile_pool(name="chunk", bufs=GROUPS * CHUNKS))
        stage = ctx.enter_context(tc.tile_pool(name="stage", bufs=5))
        turn_psum = ctx.enter_context(tc.psum_pool(name="turn_psum", bufs=2))
        field_psum = ctx.enter_context(tc.psum_pool(name="field_psum", bufs=2))
        overlap_psum = ctx.enter_context(tc.psum_pool(name="overlap_psum", bufs=CHUNKS))

        ctx.enter_context(tc.manual_schedule())

        warm = keep.tile([P, 1], F32, name="warm")
        nc.gpsimd.memset(warm[:], 0.0)
        nc.scalar.activation(warm[:], warm[:], TANH)
        ident = keep.tile([P, P], F32, name="ident")
        make_identity(nc, ident[:])

        scales = keep.tile([P, SITES], F32, name="scales")
        b16 = keep.tile([P, TILES], BF16, name="b16")
        c16 = keep.tile([P, TILES], BF16, name="c16")
        b32 = keep.tile([P, TILES], F32, name="b32")
        c32 = keep.tile([P, TILES], F32, name="c32")

        j_codes = {}
        m_raw = {}
        m_mixed = {}
        m_mx, m_mx_scale = {}, {}
        j_scaled = {}
        words_psum = {}
        j_turned = {}
        j_mx, j_mx_scale = {}, {}
        h_psum = {}
        v = {}
        g = {}
        g_mixed = {}
        g_mx, g_mx_scale = {}, {}

        def load_j(n):
            tile = code_pool.tile([P, SITES], U8, name="j_bytes")
            rows = J_bytes.rearrange("(G p t) j -> G t p j", p=P, t=PACK)
            nc.sync.dma_start(out=tile[:], in_=rows[n // PACK, n % PACK])
            j_codes[n] = tile

        def load_scales(part):
            cols = slice(part * SITES // 4, (part + 1) * SITES // 4)
            row = J_scale.rearrange("o j -> (o j)")
            nc.sync.dma_start(out=scales[:, cols], in_=row[cols].partition_broadcast(P))

        def load_m(k):
            tile = m_pool.tile([P, PACK, REPLICAS], BF16, name="m_rows", align_bytes=64)
            nc.sync.dma_start(out=tile[:], in_=m.rearrange("(k p t) a -> k p t a", p=P, t=PACK)[k])
            m_raw[k] = tile

        def load_sites(tile16, vector):
            nc.sync.dma_start(
                out=tile16[:].rearrange("p (G t) -> p G t", t=PACK),
                in_=vector.rearrange("(G p t) -> p G t", p=P, t=PACK),
            )

        load_j(0)
        for part in range(4):
            load_scales(part)
        load_j(1)
        load_m(0)
        load_m(1)
        load_j(2)
        load_m(2)
        load_m(3)
        load_sites(b16, b)
        load_sites(c16, c)
        for n in range(3, TILES):
            load_j(n)
        nc.gpsimd.tensor_copy(out=b32[:], in_=b16[:])
        nc.gpsimd.tensor_copy(out=c32[:], in_=c16[:])

        def copy(out_ap, in_ap, on_vector):
            if on_vector:
                nc.vector.tensor_copy(out=out_ap, in_=in_ap)
            else:
                nc.scalar.copy(out_ap, in_ap)

        def interleave(mixed, rows, on_vector):
            copy(
                mixed.rearrange("p (w i t) -> p w t i", i=NEAR, t=PACK),
                rows.rearrange("p t (w i) -> p w t i", i=NEAR),
                on_vector,
            )

        def quantise(codes, code_scales, mixed):
            nc.vector.quantize_mx(out=codes.bitcast(FP8X4), scales=code_scales, in_=mixed)

        def matmul_mx(acc, lhsT, lhsT_scale, rhs, rhs_scale, start, stop):
            nc.tensor.matmul_mx(
                out=acc,
                lhsT=lhsT.bitcast(FP8X4),
                lhsT_scale=lhsT_scale,
                rhs=rhs.bitcast(FP8X4),
                rhs_scale=rhs_scale,
                start=start,
                stop=stop,
            )

        def interleave_m(k):
            tile = m_pool.tile([P, PACK * REPLICAS], BF16, name="m_mixed", align_bytes=64)
            interleave(tile[:], m_raw[k][:], on_vector=False)
            m_mixed[k] = tile

        def quantise_m(k):
            codes = m_pool.tile([P, REPLICAS], U32, name="m_codes", align_bytes=64)
            code_scales = m_pool.tile([P, REPLICAS], U8, name="m_scales", align_bytes=64)
            quantise(codes[:], code_scales[:], m_mixed[k][:])
            m_mx[k], m_mx_scale[k] = codes, code_scales

        def multiply(n):
            tile = scaled_pool.tile([P, SITES], BF16, name="j_scaled")
            parts = 4 if n == 0 else 1
            for part in range(parts):
                cols = slice(part * SITES // parts, (part + 1) * SITES // parts)
                nc.vector.tensor_tensor(tile[:, cols], j_codes[n][:, cols].bitcast(FP8), scales[:, cols], op=MULT)
            j_scaled[n] = tile

        def turn(n, half):
            words = j_scaled[n][:].bitcast(F32)
            bank = turn_psum.tile([P, 4, P], F32, name="turn_bank")
            for k in range(2):
                first = (2 * half + k) * WORDS
                for u in range(2):
                    nc.tensor.transpose(bank[:, 2 * k + u, :], words[:, first + u : first + WORDS : 2], ident[:])
            words_psum[n, half] = bank

        def empty(n, half):
            if half == 0:
                tile = turned_pool.tile([P, PASSES * PASS_COLS], BF16, name="j_turned", align_bytes=64)
                j_turned[n] = tile
            words = j_turned[n][:].bitcast(F32)[:, half * 2 * WORDS : (half + 1) * 2 * WORDS]
            nc.scalar.copy(
                words.rearrange("p (k r u) -> p k r u", r=P, u=2),
                words_psum[n, half][:].rearrange("p (k u) r -> p k r u", u=2),
            )

        def quantise_j(n):
            codes = code_pool.tile([P, PASSES * P], U32, name="j_codes", align_bytes=64)
            code_scales = code_pool.tile([P, PASSES * P], U8, name="j_scales", align_bytes=64)
            quantise(codes[:], code_scales[:], j_turned[n][:])
            j_mx[n], j_mx_scale[n] = codes, code_scales

        def field(n):
            bank = field_psum.tile([P, REPLICAS], F32, name="field_bank")
            for k in range(PASSES):
                rows = slice(k * P, (k + 1) * P)
                matmul_mx(
                    bank[:],
                    j_mx[n][:, rows],
                    j_mx_scale[n][:, rows],
                    m_mx[k][:],
                    m_mx_scale[k][:],
                    start=(k == 0),
                    stop=(k == PASSES - 1),
                )
            h_psum[n] = bank

        def replicas(part, parts):
            return slice(part * REPLICAS // parts, (part + 1) * REPLICAS // parts)

        def apply_tanh(n, part, parts):
            if part == 0:
                tile = stage.tile([P, REPLICAS], F32, name="v")
                v[n] = tile
            cols = replicas(part, parts)
            nc.scalar.activation(v[n][:, cols], h_psum[n][:, cols], TANH, bias=b32[:, n : n + 1])

        def weigh(n, part, parts):
            group, t = n // PACK, n % PACK
            if group not in g:
                tile = group_pool.tile([P, PACK, REPLICAS], BF16, name="g", align_bytes=64)
                g[group] = tile
            cols = replicas(part, parts)
            if n >= FIRST_TILE_WEIGHED_ON_VECTOR:
                nc.vector.tensor_scalar(g[group][:, t, cols], v[n][:, cols], c32[:, n : n + 1], None, op0=MULT)
            else:
                nc.scalar.activation(g[group][:, t, cols], v[n][:, cols], COPY, scale=c32[:, n : n + 1])

        def interleave_g(group, chunk, on_vector):
            tile = chunk_pool.tile([P, PACK * P], BF16, name="g_mixed", align_bytes=64)
            interleave(tile[:], g[group][:, :, chunk * P : (chunk + 1) * P], on_vector)
            g_mixed[group, chunk] = tile

        def quantise_g(group, chunk):
            codes = chunk_pool.tile([P, P], U32, name="g_codes", align_bytes=64)
            code_scales = chunk_pool.tile([P, P], U8, name="g_scales", align_bytes=64)
            quantise(codes[:], code_scales[:], g_mixed[group, chunk][:])
            g_mx[group, chunk], g_mx_scale[group, chunk] = codes, code_scales

        overlap_banks = [overlap_psum.tile([P, REPLICAS], F32, name="overlap_bank") for chunk in range(CHUNKS)]

        def overlap(group, chunk):
            matmul_mx(
                overlap_banks[chunk][:],
                g_mx[group, chunk][:],
                g_mx_scale[group, chunk][:],
                m_mx[group][:],
                m_mx_scale[group][:],
                start=(group == 0),
                stop=(group == GROUPS - 1),
            )

        def finish(chunk):
            result = stage.tile([P, REPLICAS], F32, name="result")
            copy(result[:], overlap_banks[chunk][:], on_vector=(chunk % 2 == 1))
            nc.sync.dma_start(out=out[chunk * P : (chunk + 1) * P, :], in_=result[:])

        tasks = []

        def at(slot, task, *args):
            tasks.append((slot, len(tasks), task, args))

        for k in range(PASSES):
            at(SLOT_INTERLEAVE_M[k], interleave_m, k)
            at(SLOT_INTERLEAVE_M[k] + LAG_QUANTISE_M, quantise_m, k)
        for n in range(TILES):
            at(n + LAG_MULTIPLY, multiply, n)
            for half in range(2):
                at(n + LAG_TURN + half * LAG_SECOND_HALF, turn, n, half)
                at(n + LAG_TURN + half * LAG_SECOND_HALF, empty, n, half)
            at(n + LAG_QUANTISE, quantise_j, n)
            at(n + LAG_FIELD, field, n)
            parts = 2 if n == TILES - 1 else 1
            for part in range(parts):
                at(n + LAG_TANH, apply_tanh, n, part, parts)
                at(n + LAG_WEIGH, weigh, n, part, parts)
        for chunk in range(CHUNKS):
            for group in range(GROUPS - 1):
                slot = group * PACK + PACK - 1 + chunk * CHUNK_STEP
                at(slot + LAG_INTERLEAVE, interleave_g, group, chunk, chunk in CHUNKS_INTERLEAVED_ON_VECTOR)
                at(slot + LAG_QUANTISE_G, quantise_g, group, chunk)
                at(slot + LAG_OVERLAP, overlap, group, chunk)
            at(SLOT_END, interleave_g, GROUPS - 1, chunk, chunk in LAST_CHUNKS_INTERLEAVED_ON_VECTOR)
            at(SLOT_END + 1, quantise_g, GROUPS - 1, chunk)
            at(SLOT_END + 1, overlap, GROUPS - 1, chunk)
        for chunk in range(CHUNKS):
            at(SLOT_END + 2, finish, chunk)
        for slot, order, task, args in sorted(tasks, key=lambda entry: entry[:2]):
            task(*args)
